import numpy as np
import ml_dtypes


def mxq(x, axis, fmt="e4m3"):
    dtype, down = {"e4m3": (ml_dtypes.float8_e4m3fn, 7), "e5m2": (ml_dtypes.float8_e5m2, 14)}[fmt]
    v = np.moveaxis(np.asarray(x, np.float32).astype(ml_dtypes.bfloat16).astype(np.float64), axis, -1)
    blocks = v.reshape(v.shape[:-1] + (-1, 32))
    amax = np.abs(blocks).max(-1, keepdims=True)
    byte = np.maximum(np.where(amax > 0, np.frexp(amax)[1] - 1 + 127, 0) - down, 1)
    scale = np.exp2(byte - 127.0)
    codes = (blocks / scale).astype(np.float32).astype(dtype).astype(np.float64)
    return np.moveaxis((codes * scale).reshape(v.shape), -1, axis)


WIDE = False


def mx_kscale(k):
    if not WIDE:
        return np.ones(k)
    levels = np.array([10, -10, 5, -5, 0])
    if k % 512:
        return np.exp2(np.random.permutation(np.resize(levels, k // 32))).repeat(32)
    a = np.empty((k // 512, 16))
    for p in range(k // 512):
        a[p, :8] = np.random.permutation(np.resize(levels, 8))
        for g in range(8):
            far = levels[np.abs(levels - a[p, g]) >= 10]
            a[p, g + 8] = far[np.random.randint(len(far))]
    return np.exp2(a.ravel()).repeat(32)


def f64(x):
    return np.asarray(x).astype(np.float64)


def striped(idx):
    return np.tile(idx.reshape(-1, 16).T, (8, 1)).astype(np.uint16)


def unstriped(offs):
    return offs[:16].T.reshape(-1).astype(np.int64)


K, T, E, C, N = 1024, 2048, 4, 256, 256


def by_expert(wq, xq):
    return np.concatenate([wq[e].T @ xq[:, e * C:(e + 1) * C] for e in range(E)], axis=1)


def setup_inputs():
    n = np.random.standard_normal
    s = mx_kscale(K)[:, None]
    return {
        "xT": (n((K, T)) * s).astype(np.float32),
        "w": (n((E, K, N)) / np.sqrt(K) / s[None]).astype(np.float32),
        "offs": striped(np.random.permutation(T)[:E * C]),
    }


def reference(xT, w, offs):
    idx = unstriped(offs)
    xq = mxq(f64(xT)[:, idx], 0, "e4m3")
    y = by_expert(mxq(f64(w), 1, "e4m3"), xq)
    out = np.zeros((N, T))
    out[:, idx] = y
    return out

@@ -1,0 +1,139 @@
+from contextlib import ExitStack
+
+import concourse.mybir as mybir
+
+K, T, E, C, N = 1024, 2048, 4, 256, 256
+FLOPS = 2 * K * N * E * C
+
+F32 = mybir.dt.float32
+BF16 = mybir.dt.bfloat16
+U32 = mybir.dt.uint32
+U16 = mybir.dt.uint16
+U8 = mybir.dt.uint8
+FP8X4 = mybir.dt.float8_e4m3fn_x4
+
+P = 128
+PASSES = K // 512
+SLOTS = E * C
+BLOCKS = N // P
+
+CHUNKS_EARLY = ((0, 1024, 768), (1024, 1024, 768))
+CHUNKS_THIRD = ((0, 1024, 896), (1024, 1024, 896))
+CHUNKS_LAST = ((0, 1024, 896), (1024, 512, 448), (1536, 512, 448))
+QUANT_CUTS = (((0, 1024),), ((0, 256), (256, 256), (512, 512)))
+SCATTER_GROUPS = ((0, 1), (1, 1), (2, 2))
+
+
+def tile_routed_moe_kernel(tc, xT, w, offs, out):
+    nc = tc.nc
+    with ExitStack() as ctx:
+        held = ctx.enter_context(tc.tile_pool(name="held", bufs=1))
+        psum = ctx.enter_context(tc.psum_pool(name="psum", bufs=1))
+
+        offsets = held.tile([P, SLOTS // 16], U16, name="offsets")
+        nc.sync.dma_start(offsets[:], offs)
+
+        units = [(g, u) for g in range(PASSES) for u in range(2)]
+        last_unit = units[-1]
+        x_view = xT.rearrange("(g p t) n -> g p t n", p=P, t=4)
+
+        w_raw = [held.tile([P, PASSES, 4, N], F32, name="w_raw%d" % e, tag="w_raw%d" % e) for e in range(E)]
+        raw = dict((gu, held.tile([P, 2, T], F32, name="raw%d%d" % gu)) for gu in units)
+
+        def load_w(e):
+            nc.sync.dma_start(w_raw[e][:], w[e].rearrange("(g p j) n -> p g j n", p=P, j=4))
+
+        load_w(0)
+        for gu in units:
+            g, u = gu
+            for c0, cw, sc in CHUNKS_LAST if gu == last_unit else (CHUNKS_THIRD if g == PASSES - 1 else CHUNKS_EARLY):
+                nc.sync.dma_start(raw[gu][:, :, c0 : c0 + cw], x_view[g, :, 2 * u : 2 * u + 2, c0 : c0 + cw])
+        for e in range(1, E):
+            load_w(e)
+
+        window = [held.tile([P, T], F32, name="window%d" % b) for b in range(BLOCKS)]
+        for b in range(BLOCKS):
+            nc.vector.memset(window[b][:], 0.0)
+
+        w_grouped = [held.tile([P, PASSES, N, 4], BF16, name="w_grouped%d" % e, align_bytes=64) for e in range(E)]
+        w_codes = [held.tile([P, PASSES * N], U32, name="w_codes%d" % e, align_bytes=64) for e in range(E)]
+        w_scales = [held.tile([P, PASSES * N], U8, name="w_scales%d" % e, align_bytes=64) for e in range(E)]
+
+        def group_w(e):
+            nc.scalar.copy(
+                out=w_grouped[e][:].rearrange("p g (c i) j -> p g c j i", i=4),
+                in_=w_raw[e][:].rearrange("p g j (c i) -> p g c j i", i=4),
+            )
+
+        def quantize_w(e):
+            nc.vector.quantize_mx(
+                out=w_codes[e][:].bitcast(FP8X4),
+                scales=w_scales[e][:],
+                in_=w_grouped[e][:].rearrange("p g n j -> p (g n j)"),
+            )
+
+        group_w(0)
+        quantize_w(0)
+
+        pair = dict((gu, held.tile([P, T, 2], BF16, name="pair%d%d" % gu)) for gu in units)
+        grouped = [held.tile([P, SLOTS, 4], BF16, name="grouped%d" % g, align_bytes=64) for g in range(PASSES)]
+        x_codes = [held.tile([P, SLOTS], U32, name="x_codes%d" % g, align_bytes=64) for g in range(PASSES)]
+        x_scales = [held.tile([P, SLOTS], U8, name="x_scales%d" % g, align_bytes=64) for g in range(PASSES)]
+
+        for gu in units:
+            g, u = gu
+            for c0, cw, sc in CHUNKS_LAST if gu == last_unit else (CHUNKS_THIRD if g == PASSES - 1 else CHUNKS_EARLY):
+                nc.scalar.copy(
+                    out=pair[gu][:, c0 : c0 + sc, :],
+                    in_=raw[gu][:, :, c0 : c0 + sc].rearrange("p e n -> p n e"),
+                )
+                nc.vector.tensor_copy(
+                    out=pair[gu][:, c0 + sc : c0 + cw, :],
+                    in_=raw[gu][:, :, c0 + sc : c0 + cw].rearrange("p e n -> p n e"),
+                )
+            words = pair[gu][:].rearrange("p n e -> p (n e)").bitcast(U32)
+            slot_words = grouped[g][:].rearrange("p s t -> p (s t)").bitcast(U32).rearrange("p (s u) -> p s u", u=2)
+            nc.vector.tensor_copy(out=slot_words[:, :, u], in_=words.indirect(offsets[:]))
+            if u == 1:
+                for s0, sn in QUANT_CUTS[g]:
+                    nc.vector.quantize_mx(
+                        out=x_codes[g][:, s0 : s0 + sn].bitcast(FP8X4),
+                        scales=x_scales[g][:, s0 : s0 + sn],
+                        in_=grouped[g][:, s0 : s0 + sn, :].rearrange("p s t -> p (s t)"),
+                    )
+
+        y = dict()
+        y_whole = dict()
+        for e in range(E):
+            if e + 1 < E:
+                group_w(e + 1)
+            if e > 0:
+                quantize_w(e)
+            for first, count in SCATTER_GROUPS:
+                if e == first:
+                    y_group = held.tile([P, BLOCKS, count * C], F32, name="y%d" % first, tag="w_raw%d" % (first + 1))
+                    for member in range(count):
+                        y[first + member] = y_group[:, :, member * C : (member + 1) * C]
+                    y_whole[first] = y_group
+            for b in range(BLOCKS):
+                acc = psum.tile([P, C], F32, name="acc%d%d" % (e, b))
+                for g in range(PASSES):
+                    cols = slice(g * N + b * P, g * N + (b + 1) * P)
+                    nc.tensor.matmul_mx(
+                        out=acc[:],
+                        lhsT=w_codes[e][:, cols].bitcast(FP8X4),
+                        lhsT_scale=w_scales[e][:, cols],
+                        rhs=x_codes[g][:, e * C : (e + 1) * C].bitcast(FP8X4),
+                        rhs_scale=x_scales[g][:, e * C : (e + 1) * C],
+                        start=(g == 0),
+                        stop=(g == PASSES - 1),
+                    )
+                nc.scalar.copy(out=y[e][:, b, :], in_=acc[:])
+        for first, count in SCATTER_GROUPS:
+            for b in range(BLOCKS):
+                nc.vector.tensor_copy(
+                    out=window[b][:].indirect(offsets[:, first * C // 16 : (first + count) * C // 16]),
+                    in_=y_whole[first][:, b, :],
+                )
+        for b in range(BLOCKS):
+            nc.sync.dma_start(out[b * P : (b + 1) * P, :], window[b][:])

@@ -17,11 +17,11 @@ PASSES = K // 512
 SLOTS = E * C
 BLOCKS = N // P
 
-CHUNKS_EARLY = ((0, 1024, 768), (1024, 1024, 768))
-CHUNKS_THIRD = ((0, 1024, 896), (1024, 1024, 896))
-CHUNKS_LAST = ((0, 1024, 896), (1024, 512, 448), (1536, 512, 448))
+CHUNKS_EARLY = ((0, 1024, 1024), (1024, 1024, 1024))
+CHUNKS_THIRD = ((0, 1024, 1024), (1024, 1024, 1024))
+CHUNKS_LAST = ((0, 1024, 1024), (1024, 512, 512), (1536, 512, 512))
 QUANT_CUTS = (((0, 1024),), ((0, 256), (256, 256), (512, 512)))
-SCATTER_GROUPS = ((0, 1), (1, 1), (2, 2))
+SCATTER_ORDER = ((0, 0), (0, 1), (1, 0), (1, 1), (2, 0), (3, 0), (2, 1), (3, 1))
 
 
 def tile_routed_moe_kernel(tc, xT, w, offs, out):
@@ -37,48 +37,63 @@ def tile_routed_moe_kernel(tc, xT, w, offs, out):
         last_unit = units[-1]
         x_view = xT.rearrange("(g p t) n -> g p t n", p=P, t=4)
 
-        w_raw = [held.tile([P, PASSES, 4, N], F32, name="w_raw%d" % e, tag="w_raw%d" % e) for e in range(E)]
+        halves = [(e, g) for e in range(E) for g in range(PASSES)]
+        w_raw = dict((eg, held.tile([P, 4, N], F32, name="w_raw%d%d" % eg, tag="w_raw%d%d" % eg)) for eg in halves)
         raw = dict((gu, held.tile([P, 2, T], F32, name="raw%d%d" % gu)) for gu in units)
 
-        def load_w(e):
-            nc.sync.dma_start(w_raw[e][:], w[e].rearrange("(g p j) n -> p g j n", p=P, j=4))
-
-        load_w(0)
         for gu in units:
             g, u = gu
             for c0, cw, sc in CHUNKS_LAST if gu == last_unit else (CHUNKS_THIRD if g == PASSES - 1 else CHUNKS_EARLY):
                 nc.sync.dma_start(raw[gu][:, :, c0 : c0 + cw], x_view[g, :, 2 * u : 2 * u + 2, c0 : c0 + cw])
-        for e in range(1, E):
-            load_w(e)
+        for e, g in halves:
+            nc.sync.dma_start(w_raw[(e, g)][:], w[e].rearrange("(g p j) n -> g p j n", p=P, j=4)[g])
 
         window = [held.tile([P, T], F32, name="window%d" % b) for b in range(BLOCKS)]
         for b in range(BLOCKS):
             nc.vector.memset(window[b][:], 0.0)
 
-        w_grouped = [held.tile([P, PASSES, N, 4], BF16, name="w_grouped%d" % e, align_bytes=64) for e in range(E)]
-        w_codes = [held.tile([P, PASSES * N], U32, name="w_codes%d" % e, align_bytes=64) for e in range(E)]
+        w_grouped = [
+            held.tile([P, PASSES, N, 4], BF16, name="w_grouped%d" % e, tag="w_grouped%d" % e, align_bytes=64) for e in range(E)
+        ]
+        w_codes = [
+            held.tile([P, PASSES * N], U32, name="w_codes%d" % e, tag="w_codes%d" % e, align_bytes=64) for e in range(E)
+        ]
         w_scales = [held.tile([P, PASSES * N], U8, name="w_scales%d" % e, align_bytes=64) for e in range(E)]
 
-        def group_w(e):
+        def group_w(e, g):
             nc.scalar.copy(
-                out=w_grouped[e][:].rearrange("p g (c i) j -> p g c j i", i=4),
-                in_=w_raw[e][:].rearrange("p g j (c i) -> p g c j i", i=4),
+                out=w_grouped[e][:, g].rearrange("p (c i) j -> p c j i", i=4),
+                in_=w_raw[(e, g)][:].rearrange("p j (c i) -> p c j i", i=4),
             )
 
-        def quantize_w(e):
+        def quantize_w(e, g0, gn):
             nc.vector.quantize_mx(
-                out=w_codes[e][:].bitcast(FP8X4),
-                scales=w_scales[e][:],
-                in_=w_grouped[e][:].rearrange("p g n j -> p (g n j)"),
+                out=w_codes[e][:, g0 * N : (g0 + gn) * N].bitcast(FP8X4),
+                scales=w_scales[e][:, g0 * N : (g0 + gn) * N],
+                in_=w_grouped[e][:, g0 : g0 + gn].rearrange("p g n j -> p (g n j)"),
             )
-
-        group_w(0)
-        quantize_w(0)
 
         pair = dict((gu, held.tile([P, T, 2], BF16, name="pair%d%d" % gu)) for gu in units)
         grouped = [held.tile([P, SLOTS, 4], BF16, name="grouped%d" % g, align_bytes=64) for g in range(PASSES)]
         x_codes = [held.tile([P, SLOTS], U32, name="x_codes%d" % g, align_bytes=64) for g in range(PASSES)]
         x_scales = [held.tile([P, SLOTS], U8, name="x_scales%d" % g, align_bytes=64) for g in range(PASSES)]
+
+        def codes_of(g, s0, sn):
+            if g < PASSES - 1:
+                return x_codes[g][:, s0 : s0 + sn]
+            if s0 < C:
+                return x_codes[g][:, s0 : s0 + sn]
+            return x_codes_rest[0][:, s0 - C : s0 - C + sn]
+
+        def quantize_x(g, cut):
+            s0, sn = cut
+            nc.vector.quantize_mx(
+                out=codes_of(g, s0, sn).bitcast(FP8X4),
+                scales=x_scales[g][:, s0 : s0 + sn],
+                in_=grouped[g][:, s0 : s0 + sn, :].rearrange("p s t -> p (s t)"),
+            )
+
+        x_codes_rest = []
 
         for gu in units:
             g, u = gu
@@ -87,53 +102,74 @@ def tile_routed_moe_kernel(tc, xT, w, offs, out):
                     out=pair[gu][:, c0 : c0 + sc, :],
                     in_=raw[gu][:, :, c0 : c0 + sc].rearrange("p e n -> p n e"),
                 )
-                nc.vector.tensor_copy(
-                    out=pair[gu][:, c0 + sc : c0 + cw, :],
-                    in_=raw[gu][:, :, c0 + sc : c0 + cw].rearrange("p e n -> p n e"),
-                )
+                if sc < cw:
+                    nc.vector.tensor_copy(
+                        out=pair[gu][:, c0 + sc : c0 + cw, :],
+                        in_=raw[gu][:, :, c0 + sc : c0 + cw].rearrange("p e n -> p n e"),
+                    )
             words = pair[gu][:].rearrange("p n e -> p (n e)").bitcast(U32)
             slot_words = grouped[g][:].rearrange("p s t -> p (s t)").bitcast(U32).rearrange("p (s u) -> p s u", u=2)
             nc.vector.tensor_copy(out=slot_words[:, :, u], in_=words.indirect(offsets[:]))
             if u == 1:
-                for s0, sn in QUANT_CUTS[g]:
-                    nc.vector.quantize_mx(
-                        out=x_codes[g][:, s0 : s0 + sn].bitcast(FP8X4),
-                        scales=x_scales[g][:, s0 : s0 + sn],
-                        in_=grouped[g][:, s0 : s0 + sn, :].rearrange("p s t -> p (s t)"),
-                    )
+                quantize_x(g, QUANT_CUTS[g][0])
 
+        acc = dict()
         y = dict()
-        y_whole = dict()
-        for e in range(E):
-            if e + 1 < E:
-                group_w(e + 1)
-            if e > 0:
-                quantize_w(e)
-            for first, count in SCATTER_GROUPS:
-                if e == first:
-                    y_group = held.tile([P, BLOCKS, count * C], F32, name="y%d" % first, tag="w_raw%d" % (first + 1))
-                    for member in range(count):
-                        y[first + member] = y_group[:, :, member * C : (member + 1) * C]
-                    y_whole[first] = y_group
+
+        def multiply(e):
             for b in range(BLOCKS):
-                acc = psum.tile([P, C], F32, name="acc%d%d" % (e, b))
+                acc[(e, b)] = psum.tile([P, C], F32, name="acc%d%d" % (e, b))
                 for g in range(PASSES):
                     cols = slice(g * N + b * P, g * N + (b + 1) * P)
                     nc.tensor.matmul_mx(
-                        out=acc[:],
+                        out=acc[(e, b)][:],
                         lhsT=w_codes[e][:, cols].bitcast(FP8X4),
                         lhsT_scale=w_scales[e][:, cols],
-                        rhs=x_codes[g][:, e * C : (e + 1) * C].bitcast(FP8X4),
+                        rhs=codes_of(g, e * C, C).bitcast(FP8X4),
                         rhs_scale=x_scales[g][:, e * C : (e + 1) * C],
                         start=(g == 0),
                         stop=(g == PASSES - 1),
                     )
-                nc.scalar.copy(out=y[e][:, b, :], in_=acc[:])
-        for first, count in SCATTER_GROUPS:
-            for b in range(BLOCKS):
-                nc.vector.tensor_copy(
-                    out=window[b][:].indirect(offsets[:, first * C // 16 : (first + count) * C // 16]),
-                    in_=y_whole[first][:, b, :],
-                )
+
+        def copy_out(e, b, tag, align):
+            if align:
+                y[(e, b)] = held.tile([P, C], F32, name="y%d%d" % (e, b), tag=tag, align_bytes=align)
+            else:
+                y[(e, b)] = held.tile([P, C], F32, name="y%d%d" % (e, b), tag=tag)
+            nc.scalar.copy(out=y[(e, b)][:], in_=acc[(e, b)][:])
+
+        for g in range(PASSES):
+            group_w(0, g)
+            quantize_w(0, g, 1)
+        x_codes_rest.append(held.tile([P, SLOTS - C], U32, name="x_codes_rest", tag="w_grouped0", align_bytes=64))
+        for cut in QUANT_CUTS[PASSES - 1][1:]:
+            quantize_x(PASSES - 1, cut)
+        group_w(1, 0)
+        multiply(0)
+        copy_out(0, 0, "y00", 0)
+        group_w(1, 1)
+        copy_out(0, 1, "w_raw11", 0)
+        quantize_w(1, 0, PASSES)
+        group_w(2, 0)
+        multiply(1)
+        copy_out(1, 0, "y10", 0)
+        group_w(2, 1)
+        copy_out(1, 1, "w_raw21", 0)
+        quantize_w(2, 0, PASSES)
+        group_w(3, 0)
+        group_w(3, 1)
+        multiply(2)
+        copy_out(2, 0, "w_raw31", 0)
+        quantize_w(3, 0, PASSES)
+        multiply(3)
+        copy_out(3, 0, "y30", 0)
+        copy_out(2, 1, "w_codes3", 64)
+        copy_out(3, 1, "y31", 0)
+
+        for e, b in SCATTER_ORDER:
+            nc.vector.tensor_copy(
+                out=window[b][:].indirect(offsets[:, e * C // 16 : (e + 1) * C // 16]),
+                in_=y[(e, b)][:],
+            )
         for b in range(BLOCKS):
             nc.sync.dma_start(out[b * P : (b + 1) * P, :], window[b][:])

@@ -19,7 +19,7 @@ BLOCKS = N // P
 
 CHUNKS_EARLY = ((0, 1024, 1024), (1024, 1024, 1024))
 CHUNKS_THIRD = ((0, 1024, 1024), (1024, 1024, 1024))
-CHUNKS_LAST = ((0, 1024, 1024), (1024, 512, 512), (1536, 512, 512))
+CHUNKS_LAST = ((0, 1024, 1024), (1024, 512, 512), (1536, 256, 256), (1792, 256, 256))
 QUANT_CUTS = (((0, 1024),), ((0, 256), (256, 256), (512, 512)))
 SCATTER_ORDER = ((0, 0), (0, 1), (1, 0), (1, 1), (2, 0), (3, 0), (2, 1), (3, 1))
 
@@ -75,15 +75,13 @@ def tile_routed_moe_kernel(tc, xT, w, offs, out):
 
         pair = dict((gu, held.tile([P, T, 2], BF16, name="pair%d%d" % gu)) for gu in units)
         grouped = [held.tile([P, SLOTS, 4], BF16, name="grouped%d" % g, align_bytes=64) for g in range(PASSES)]
-        x_codes = [held.tile([P, SLOTS], U32, name="x_codes%d" % g, align_bytes=64) for g in range(PASSES)]
+        x_codes = [held.tile([P, SLOTS], U32, name="x_codes%d" % g, align_bytes=64) for g in range(PASSES - 1)]
         x_scales = [held.tile([P, SLOTS], U8, name="x_scales%d" % g, align_bytes=64) for g in range(PASSES)]
 
         def codes_of(g, s0, sn):
             if g < PASSES - 1:
                 return x_codes[g][:, s0 : s0 + sn]
-            if s0 < C:
-                return x_codes[g][:, s0 : s0 + sn]
-            return x_codes_rest[0][:, s0 - C : s0 - C + sn]
+            return x_codes_last[0][:, s0 : s0 + sn]
 
         def quantize_x(g, cut):
             s0, sn = cut
@@ -93,7 +91,7 @@ def tile_routed_moe_kernel(tc, xT, w, offs, out):
                 in_=grouped[g][:, s0 : s0 + sn, :].rearrange("p s t -> p (s t)"),
             )
 
-        x_codes_rest = []
+        x_codes_last = []
 
         for gu in units:
             g, u = gu
@@ -110,8 +108,9 @@ def tile_routed_moe_kernel(tc, xT, w, offs, out):
             words = pair[gu][:].rearrange("p n e -> p (n e)").bitcast(U32)
             slot_words = grouped[g][:].rearrange("p s t -> p (s t)").bitcast(U32).rearrange("p (s u) -> p s u", u=2)
             nc.vector.tensor_copy(out=slot_words[:, :, u], in_=words.indirect(offsets[:]))
-            if u == 1:
-                quantize_x(g, QUANT_CUTS[g][0])
+            if u == 1 and g < PASSES - 1:
+                for cut in QUANT_CUTS[g]:
+                    quantize_x(g, cut)
 
         acc = dict()
         y = dict()
@@ -140,9 +139,9 @@ def tile_routed_moe_kernel(tc, xT, w, offs, out):
 
         for g in range(PASSES):
             group_w(0, g)
-            quantize_w(0, g, 1)
-        x_codes_rest.append(held.tile([P, SLOTS - C], U32, name="x_codes_rest", tag="w_grouped0", align_bytes=64))
-        for cut in QUANT_CUTS[PASSES - 1][1:]:
+        quantize_w(0, 0, PASSES)
+        x_codes_last.append(held.tile([P, SLOTS], U32, name="x_codes_last", tag="w_grouped0", align_bytes=64))
+        for cut in QUANT_CUTS[PASSES - 1]:
             quantize_x(PASSES - 1, cut)
         group_w(1, 0)
         multiply(0)

@@ -19,7 +19,7 @@ BLOCKS = N // P
 
 CHUNKS_EARLY = ((0, 1024, 1024), (1024, 1024, 1024))
 CHUNKS_THIRD = ((0, 1024, 1024), (1024, 1024, 1024))
-CHUNKS_LAST = ((0, 1024, 1024), (1024, 512, 512), (1536, 256, 256), (1792, 256, 256))
+CHUNKS_LAST = ((0, 1024, 1024), (1024, 512, 512), (1536, 512, 512))
 QUANT_CUTS = (((0, 1024),), ((0, 256), (256, 256), (512, 512)))
 SCATTER_ORDER = ((0, 0), (0, 1), (1, 0), (1, 1), (2, 0), (3, 0), (2, 1), (3, 1))
 

@@ -17,9 +17,9 @@ PASSES = K // 512
 SLOTS = E * C
 BLOCKS = N // P
 
-CHUNKS_EARLY = ((0, 1024, 1024), (1024, 1024, 1024))
-CHUNKS_THIRD = ((0, 1024, 1024), (1024, 1024, 1024))
-CHUNKS_LAST = ((0, 1024, 1024), (1024, 512, 512), (1536, 512, 512))
+CHUNKS_EARLY = ((0, 512, 448), (512, 512, 448), (1024, 512, 448), (1536, 512, 448))
+CHUNKS_THIRD = ((0, 512, 512), (512, 512, 512), (1024, 512, 512), (1536, 512, 512))
+CHUNKS_LAST = ((0, 512, 384), (512, 512, 384), (1024, 512, 512), (1536, 512, 512))
 QUANT_CUTS = (((0, 1024),), ((0, 256), (256, 256), (512, 512)))
 SCATTER_ORDER = ((0, 0), (0, 1), (1, 0), (1, 1), (2, 0), (3, 0), (2, 1), (3, 1))
 

@@ -20,8 +20,8 @@ BLOCKS = N // P
 CHUNKS_EARLY = ((0, 512, 448), (512, 512, 448), (1024, 512, 448), (1536, 512, 448))
 CHUNKS_THIRD = ((0, 512, 512), (512, 512, 512), (1024, 512, 512), (1536, 512, 512))
 CHUNKS_LAST = ((0, 512, 384), (512, 512, 384), (1024, 512, 512), (1536, 512, 512))
-QUANT_CUTS = (((0, 1024),), ((0, 256), (256, 256), (512, 512)))
-SCATTER_ORDER = ((0, 0), (0, 1), (1, 0), (1, 1), (2, 0), (3, 0), (2, 1), (3, 1))
+QUANT_CUTS = (((0, 1024),), ((0, 512), (512, 512)))
+SCATTER_ORDER = ((0, 1, 0), (0, 1, 1), (1, 1, 0), (1, 1, 1), (2, 2, 0), (2, 2, 1))
 
 
 def tile_routed_moe_kernel(tc, xT, w, offs, out):
@@ -150,25 +150,25 @@ def tile_routed_moe_kernel(tc, xT, w, offs, out):
         copy_out(0, 1, "w_raw11", 0)
         quantize_w(1, 0, PASSES)
         group_w(2, 0)
-        multiply(1)
-        copy_out(1, 0, "y10", 0)
         group_w(2, 1)
-        copy_out(1, 1, "w_raw21", 0)
+        multiply(1)
+        copy_out(1, 0, "w_raw21", 0)
         quantize_w(2, 0, PASSES)
         group_w(3, 0)
         group_w(3, 1)
-        multiply(2)
-        copy_out(2, 0, "w_raw31", 0)
+        copy_out(1, 1, "w_raw31", 0)
         quantize_w(3, 0, PASSES)
+        multiply(2)
         multiply(3)
-        copy_out(3, 0, "y30", 0)
-        copy_out(2, 1, "w_codes3", 64)
-        copy_out(3, 1, "y31", 0)
+        for b in range(BLOCKS):
+            y[(2, b)] = held.tile([P, 2 * C], F32, name="y23%d" % b)
+            for e in (2, 3):
+                nc.scalar.copy(out=y[(2, b)][:, (e - 2) * C : (e - 1) * C], in_=acc[(e, b)][:])
 
-        for e, b in SCATTER_ORDER:
+        for first, count, b in SCATTER_ORDER:
             nc.vector.tensor_copy(
-                out=window[b][:].indirect(offsets[:, e * C // 16 : (e + 1) * C // 16]),
-                in_=y[(e, b)][:],
+                out=window[b][:].indirect(offsets[:, first * C // 16 : (first + count) * C // 16]),
+                in_=y[(first, b)][:],
             )
         for b in range(BLOCKS):
             nc.sync.dma_start(out[b * P : (b + 1) * P, :], window[b][:])

@@ -19,7 +19,7 @@ BLOCKS = N // P
 
 CHUNKS_EARLY = ((0, 512, 448), (512, 512, 448), (1024, 512, 448), (1536, 512, 448))
 CHUNKS_THIRD = ((0, 512, 512), (512, 512, 512), (1024, 512, 512), (1536, 512, 512))
-CHUNKS_LAST = ((0, 512, 384), (512, 512, 384), (1024, 512, 512), (1536, 512, 512))
+CHUNKS_LAST = ((0, 512, 512), (512, 512, 512), (1024, 512, 512), (1536, 512, 256))
 QUANT_CUTS = (((0, 1024),), ((0, 512), (512, 512)))
 SCATTER_ORDER = ((0, 1, 0), (0, 1, 1), (1, 1, 0), (1, 1, 1), (2, 2, 0), (2, 2, 1))
 

@@ -31,9 +31,9 @@ def tile_routed_moe_kernel(tc, xT, w, offs, out):
         psum = ctx.enter_context(tc.psum_pool(name="psum", bufs=1))
 
         offsets = held.tile([P, SLOTS // 16], U16, name="offsets")
-        nc.sync.dma_start(offsets[:], offs)
 
         units = [(g, u) for g in range(PASSES) for u in range(2)]
+        first_unit = units[0]
         last_unit = units[-1]
         x_view = xT.rearrange("(g p t) n -> g p t n", p=P, t=4)
 
@@ -41,7 +41,11 @@ def tile_routed_moe_kernel(tc, xT, w, offs, out):
         w_raw = dict((eg, held.tile([P, 4, N], F32, name="w_raw%d%d" % eg, tag="w_raw%d%d" % eg)) for eg in halves)
         raw = dict((gu, held.tile([P, 2, T], F32, name="raw%d%d" % gu)) for gu in units)
 
-        for gu in units:
+        for e in range(2):
+            nc.sync.dma_start(raw[first_unit][:, e, :], x_view[0, :, e, :])
+            if e == 0:
+                nc.sync.dma_start(offsets[:], offs)
+        for gu in units[1:]:
             g, u = gu
             for c0, cw, sc in CHUNKS_LAST if gu == last_unit else (CHUNKS_THIRD if g == PASSES - 1 else CHUNKS_EARLY):
                 nc.sync.dma_start(raw[gu][:, :, c0 : c0 + cw], x_view[g, :, 2 * u : 2 * u + 2, c0 : c0 + cw])
@@ -73,7 +77,7 @@ def tile_routed_moe_kernel(tc, xT, w, offs, out):
                 in_=w_grouped[e][:, g0 : g0 + gn].rearrange("p g n j -> p (g n j)"),
             )
 
-        pair = dict((gu, held.tile([P, T, 2], BF16, name="pair%d%d" % gu)) for gu in units)
+        pair = dict((gu, held.tile([P, T, 2], BF16, name="pair%d%d" % gu)) for gu in units[1:])
         grouped = [held.tile([P, SLOTS, 4], BF16, name="grouped%d" % g, align_bytes=64) for g in range(PASSES)]
         x_codes = [held.tile([P, SLOTS], U32, name="x_codes%d" % g, align_bytes=64) for g in range(PASSES - 1)]
         x_scales = [held.tile([P, SLOTS], U8, name="x_scales%d" % g, align_bytes=64) for g in range(PASSES)]
@@ -93,7 +97,9 @@ def tile_routed_moe_kernel(tc, xT, w, offs, out):
 
         x_codes_last = []
 
-        for gu in units:
+        for e in range(2):
+            nc.vector.tensor_copy(out=grouped[0][:, :, e], in_=raw[first_unit][:, e, :].indirect(offsets[:]))
+        for gu in units[1:]:
             g, u = gu
             for c0, cw, sc in CHUNKS_LAST if gu == last_unit else (CHUNKS_THIRD if g == PASSES - 1 else CHUNKS_EARLY):
                 nc.scalar.copy(

@@ -17,9 +17,11 @@ PASSES = K // 512
 SLOTS = E * C
 BLOCKS = N // P
 
-CHUNKS_EARLY = ((0, 512, 448), (512, 512, 448), (1024, 512, 448), (1536, 512, 448))
-CHUNKS_THIRD = ((0, 512, 512), (512, 512, 512), (1024, 512, 512), (1536, 512, 512))
-CHUNKS_LAST = ((0, 512, 512), (512, 512, 512), (1024, 512, 512), (1536, 512, 256))
+CHUNKS = {
+    (0, 1): ((0, 1024, 1024), (1024, 1024, 512)),
+    (1, 0): ((0, 1024, 1024), (1024, 1024, 512)),
+    (1, 1): ((0, 512, 512), (512, 512, 512), (1024, 512, 512), (1536, 512, 256)),
+}
 QUANT_CUTS = (((0, 1024),), ((0, 512), (512, 512)))
 SCATTER_ORDER = ((0, 1, 0), (0, 1, 1), (1, 1, 0), (1, 1, 1), (2, 2, 0), (2, 2, 1))
 
@@ -34,7 +36,6 @@ def tile_routed_moe_kernel(tc, xT, w, offs, out):
 
         units = [(g, u) for g in range(PASSES) for u in range(2)]
         first_unit = units[0]
-        last_unit = units[-1]
         x_view = xT.rearrange("(g p t) n -> g p t n", p=P, t=4)
 
         halves = [(e, g) for e in range(E) for g in range(PASSES)]
@@ -47,7 +48,7 @@ def tile_routed_moe_kernel(tc, xT, w, offs, out):
                 nc.sync.dma_start(offsets[:], offs)
         for gu in units[1:]:
             g, u = gu
-            for c0, cw, sc in CHUNKS_LAST if gu == last_unit else (CHUNKS_THIRD if g == PASSES - 1 else CHUNKS_EARLY):
+            for c0, cw, sc in CHUNKS[gu]:
                 nc.sync.dma_start(raw[gu][:, :, c0 : c0 + cw], x_view[g, :, 2 * u : 2 * u + 2, c0 : c0 + cw])
         for e, g in halves:
             nc.sync.dma_start(w_raw[(e, g)][:], w[e].rearrange("(g p j) n -> g p j n", p=P, j=4)[g])
@@ -101,7 +102,7 @@ def tile_routed_moe_kernel(tc, xT, w, offs, out):
             nc.vector.tensor_copy(out=grouped[0][:, :, e], in_=raw[first_unit][:, e, :].indirect(offsets[:]))
         for gu in units[1:]:
             g, u = gu
-            for c0, cw, sc in CHUNKS_LAST if gu == last_unit else (CHUNKS_THIRD if g == PASSES - 1 else CHUNKS_EARLY):
+            for c0, cw, sc in CHUNKS[gu]:
                 nc.scalar.copy(
                     out=pair[gu][:, c0 : c0 + sc, :],
                     in_=raw[gu][:, :, c0 : c0 + sc].rearrange("p e n -> p n e"),

@@ -18,8 +18,8 @@ SLOTS = E * C
 BLOCKS = N // P
 
 CHUNKS = {
-    (0, 1): ((0, 1024, 1024), (1024, 1024, 512)),
-    (1, 0): ((0, 1024, 1024), (1024, 1024, 512)),
+    (0, 1): ((0, 1024, 1024), (1024, 1024, 640)),
+    (1, 0): ((0, 1024, 1024), (1024, 1024, 640)),
     (1, 1): ((0, 512, 512), (512, 512, 512), (1024, 512, 512), (1536, 512, 256)),
 }
 QUANT_CUTS = (((0, 1024),), ((0, 512), (512, 512)))
@@ -36,6 +36,7 @@ def tile_routed_moe_kernel(tc, xT, w, offs, out):
 
         units = [(g, u) for g in range(PASSES) for u in range(2)]
         first_unit = units[0]
+        last_unit = units[-1]
         x_view = xT.rearrange("(g p t) n -> g p t n", p=P, t=4)
 
         halves = [(e, g) for e in range(E) for g in range(PASSES)]
@@ -108,10 +109,14 @@ def tile_routed_moe_kernel(tc, xT, w, offs, out):
                     in_=raw[gu][:, :, c0 : c0 + sc].rearrange("p e n -> p n e"),
                 )
                 if sc < cw:
-                    nc.vector.tensor_copy(
-                        out=pair[gu][:, c0 + sc : c0 + cw, :],
-                        in_=raw[gu][:, :, c0 + sc : c0 + cw].rearrange("p e n -> p n e"),
-                    )
+                    rest = pair[gu][:, c0 + sc : c0 + cw, :]
+                    planes = raw[gu][:, :, c0 + sc : c0 + cw].rearrange("p e n -> p n e")
+                    if gu == last_unit:
+                        nc.vector.tensor_copy(out=rest, in_=planes)
+                    else:
+                        nc.gpsimd.tensor_scalar(
+                            out=rest, in0=planes, scalar1=1.0, scalar2=0.0, op0=mybir.AluOpType.mult, op1=mybir.AluOpType.add
+                        )
             words = pair[gu][:].rearrange("p n e -> p (n e)").bitcast(U32)
             slot_words = grouped[g][:].rearrange("p s t -> p (s t)").bitcast(U32).rearrange("p (s u) -> p s u", u=2)
             nc.vector.tensor_copy(out=slot_words[:, :, u], in_=words.indirect(offsets[:]))

@@ -18,9 +18,9 @@ SLOTS = E * C
 BLOCKS = N // P
 
 CHUNKS = {
-    (0, 1): ((0, 1024, 1024), (1024, 1024, 640)),
-    (1, 0): ((0, 1024, 1024), (1024, 1024, 640)),
-    (1, 1): ((0, 512, 512), (512, 512, 512), (1024, 512, 512), (1536, 512, 256)),
+    (0, 1): ((0, 1024, 640), (1024, 512, 320), (1536, 512, 256)),
+    (1, 0): ((0, 1024, 640), (1024, 1024, 576)),
+    (1, 1): ((0, 1024, 640), (1024, 640, 352), (1664, 384, 192)),
 }
 QUANT_CUTS = (((0, 1024),), ((0, 512), (512, 512)))
 SCATTER_ORDER = ((0, 1, 0), (0, 1, 1), (1, 1, 0), (1, 1, 1), (2, 2, 0), (2, 2, 1))
@@ -36,7 +36,6 @@ def tile_routed_moe_kernel(tc, xT, w, offs, out):
 
         units = [(g, u) for g in range(PASSES) for u in range(2)]
         first_unit = units[0]
-        last_unit = units[-1]
         x_view = xT.rearrange("(g p t) n -> g p t n", p=P, t=4)
 
         halves = [(e, g) for e in range(E) for g in range(PASSES)]
@@ -111,12 +110,9 @@ def tile_routed_moe_kernel(tc, xT, w, offs, out):
                 if sc < cw:
                     rest = pair[gu][:, c0 + sc : c0 + cw, :]
                     planes = raw[gu][:, :, c0 + sc : c0 + cw].rearrange("p e n -> p n e")
-                    if gu == last_unit:
-                        nc.vector.tensor_copy(out=rest, in_=planes)
-                    else:
-                        nc.gpsimd.tensor_scalar(
-                            out=rest, in0=planes, scalar1=1.0, scalar2=0.0, op0=mybir.AluOpType.mult, op1=mybir.AluOpType.add
-                        )
+                    nc.gpsimd.tensor_scalar(
+                        out=rest, in0=planes, scalar1=1.0, scalar2=0.0, op0=mybir.AluOpType.mult, op1=mybir.AluOpType.add
+                    )
             words = pair[gu][:].rearrange("p n e -> p (n e)").bitcast(U32)
             slot_words = grouped[g][:].rearrange("p s t -> p (s t)").bitcast(U32).rearrange("p (s u) -> p s u", u=2)
             nc.vector.tensor_copy(out=slot_words[:, :, u], in_=words.indirect(offsets[:]))

@@ -22,6 +22,7 @@ CHUNKS = {
     (1, 0): ((0, 1024, 640), (1024, 1024, 576)),
     (1, 1): ((0, 1024, 640), (1024, 640, 352), (1664, 384, 192)),
 }
+W_SHARE = 144
 QUANT_CUTS = (((0, 1024),), ((0, 512), (512, 512)))
 SCATTER_ORDER = ((0, 1, 0), (0, 1, 1), (1, 1, 0), (1, 1, 1), (2, 2, 0), (2, 2, 1))
 
@@ -57,6 +58,11 @@ def tile_routed_moe_kernel(tc, xT, w, offs, out):
         for b in range(BLOCKS):
             nc.vector.memset(window[b][:], 0.0)
 
+        def gpsimd_cast(dst, src):
+            nc.gpsimd.tensor_scalar(
+                out=dst, in0=src, scalar1=1.0, scalar2=0.0, op0=mybir.AluOpType.mult, op1=mybir.AluOpType.add
+            )
+
         w_grouped = [
             held.tile([P, PASSES, N, 4], BF16, name="w_grouped%d" % e, tag="w_grouped%d" % e, align_bytes=64) for e in range(E)
         ]
@@ -66,10 +72,13 @@ def tile_routed_moe_kernel(tc, xT, w, offs, out):
         w_scales = [held.tile([P, PASSES * N], U8, name="w_scales%d" % e, align_bytes=64) for e in range(E)]
 
         def group_w(e, g):
+            mine = W_SHARE if e in (0, E - 1) else N
             nc.scalar.copy(
-                out=w_grouped[e][:, g].rearrange("p (c i) j -> p c j i", i=4),
-                in_=w_raw[(e, g)][:].rearrange("p j (c i) -> p c j i", i=4),
+                out=w_grouped[e][:, g, :mine].rearrange("p (c i) j -> p c j i", i=4),
+                in_=w_raw[(e, g)][:, :, :mine].rearrange("p j (c i) -> p c j i", i=4),
             )
+            if mine < N:
+                gpsimd_cast(w_grouped[e][:, g, mine:], w_raw[(e, g)][:, :, mine:].rearrange("p j n -> p n j"))
 
         def quantize_w(e, g0, gn):
             nc.vector.quantize_mx(
@@ -110,9 +119,7 @@ def tile_routed_moe_kernel(tc, xT, w, offs, out):
                 if sc < cw:
                     rest = pair[gu][:, c0 + sc : c0 + cw, :]
                     planes = raw[gu][:, :, c0 + sc : c0 + cw].rearrange("p e n -> p n e")
-                    nc.gpsimd.tensor_scalar(
-                        out=rest, in0=planes, scalar1=1.0, scalar2=0.0, op0=mybir.AluOpType.mult, op1=mybir.AluOpType.add
-                    )
+                    gpsimd_cast(rest, planes)
             words = pair[gu][:].rearrange("p n e -> p (n e)").bitcast(U32)
             slot_words = grouped[g][:].rearrange("p s t -> p (s t)").bitcast(U32).rearrange("p (s u) -> p s u", u=2)
             nc.vector.tensor_copy(out=slot_words[:, :, u], in_=words.indirect(offsets[:]))
@@ -125,7 +132,7 @@ def tile_routed_moe_kernel(tc, xT, w, offs, out):
 
         def multiply(e):
             for b in range(BLOCKS):
-                acc[(e, b)] = psum.tile([P, C], F32, name="acc%d%d" % (e, b))
+                acc[(e, b)] = psum.tile([P, C], F32, name="acc%d%d" % (e, b), tag="acc%d%d" % (1 if e == 2 else e, b))
                 for g in range(PASSES):
                     cols = slice(g * N + b * P, g * N + (b + 1) * P)
                     nc.tensor.matmul_mx(
@@ -138,12 +145,10 @@ def tile_routed_moe_kernel(tc, xT, w, offs, out):
                         stop=(g == PASSES - 1),
                     )
 
-        def copy_out(e, b, tag, align):
-            if align:
-                y[(e, b)] = held.tile([P, C], F32, name="y%d%d" % (e, b), tag=tag, align_bytes=align)
-            else:
-                y[(e, b)] = held.tile([P, C], F32, name="y%d%d" % (e, b), tag=tag)
-            nc.scalar.copy(out=y[(e, b)][:], in_=acc[(e, b)][:])
+        def copy_out(e, b, tag):
+            sums = held.tile([P, C], F32, name="y%d%d" % (e, b), tag=tag)
+            y[(e, b)] = sums[:]
+            nc.scalar.copy(out=y[(e, b)], in_=acc[(e, b)][:])
 
         for g in range(PASSES):
             group_w(0, g)
@@ -153,30 +158,33 @@ def tile_routed_moe_kernel(tc, xT, w, offs, out):
             quantize_x(PASSES - 1, cut)
         group_w(1, 0)
         multiply(0)
-        copy_out(0, 0, "y00", 0)
+        copy_out(0, 0, "y00")
         group_w(1, 1)
-        copy_out(0, 1, "w_raw11", 0)
+        copy_out(0, 1, "w_raw11")
         quantize_w(1, 0, PASSES)
         group_w(2, 0)
         group_w(2, 1)
         multiply(1)
-        copy_out(1, 0, "w_raw21", 0)
         quantize_w(2, 0, PASSES)
         group_w(3, 0)
         group_w(3, 1)
-        copy_out(1, 1, "w_raw31", 0)
         quantize_w(3, 0, PASSES)
+        sums1 = held.tile([P, BLOCKS, C], F32, name="sums1", tag="w_raw31")
+        for b in range(BLOCKS):
+            y[(1, b)] = sums1[:, b, :]
+            nc.scalar.copy(out=y[(1, b)], in_=acc[(1, b)][:])
         multiply(2)
         multiply(3)
         for b in range(BLOCKS):
-            y[(2, b)] = held.tile([P, 2 * C], F32, name="y23%d" % b)
+            sums23 = held.tile([P, 2 * C], F32, name="y23%d" % b)
+            y[(2, b)] = sums23[:]
             for e in (2, 3):
-                nc.scalar.copy(out=y[(2, b)][:, (e - 2) * C : (e - 1) * C], in_=acc[(e, b)][:])
+                nc.scalar.copy(out=sums23[:, (e - 2) * C : (e - 1) * C], in_=acc[(e, b)][:])
 
         for first, count, b in SCATTER_ORDER:
             nc.vector.tensor_copy(
                 out=window[b][:].indirect(offsets[:, first * C // 16 : (first + count) * C // 16]),
-                in_=y[(first, b)][:],
+                in_=y[(first, b)],
             )
         for b in range(BLOCKS):
             nc.sync.dma_start(out[b * P : (b + 1) * P, :], window[b][:])

@@ -19,7 +19,7 @@ BLOCKS = N // P
 
 CHUNKS = {
     (0, 1): ((0, 1024, 640), (1024, 512, 320), (1536, 512, 256)),
-    (1, 0): ((0, 1024, 640), (1024, 1024, 576)),
+    (1, 0): ((0, 1024, 640), (1024, 512, 512), (1536, 512, 512)),
     (1, 1): ((0, 1024, 640), (1024, 640, 352), (1664, 384, 192)),
 }
 W_SHARE = 144

from contextlib import ExitStack

import concourse.mybir as mybir

K, T, E, C, N = 1024, 2048, 4, 256, 256
FLOPS = 2 * K * N * E * C

F32 = mybir.dt.float32
BF16 = mybir.dt.bfloat16
U32 = mybir.dt.uint32
U16 = mybir.dt.uint16
U8 = mybir.dt.uint8
FP8X4 = mybir.dt.float8_e4m3fn_x4

P = 128
PASSES = K // 512
SLOTS = E * C
BLOCKS = N // P

CHUNKS = {
    (0, 1): ((0, 1024, 640), (1024, 512, 320), (1536, 512, 256)),
    (1, 0): ((0, 1024, 640), (1024, 512, 512), (1536, 512, 512)),
    (1, 1): ((0, 1024, 640), (1024, 640, 352), (1664, 384, 192)),
}
W_SHARE = 144
QUANT_CUTS = (((0, 1024),), ((0, 512), (512, 512)))
SCATTER_ORDER = ((0, 1, 0), (0, 1, 1), (1, 1, 0), (1, 1, 1), (2, 2, 0), (2, 2, 1))


def tile_routed_moe_kernel(tc, xT, w, offs, out):
    nc = tc.nc
    with ExitStack() as ctx:
        held = ctx.enter_context(tc.tile_pool(name="held", bufs=1))
        psum = ctx.enter_context(tc.psum_pool(name="psum", bufs=1))

        offsets = held.tile([P, SLOTS // 16], U16, name="offsets")

        units = [(g, u) for g in range(PASSES) for u in range(2)]
        first_unit = units[0]
        x_view = xT.rearrange("(g p t) n -> g p t n", p=P, t=4)

        halves = [(e, g) for e in range(E) for g in range(PASSES)]
        w_raw = dict((eg, held.tile([P, 4, N], F32, name="w_raw%d%d" % eg, tag="w_raw%d%d" % eg)) for eg in halves)
        raw = dict((gu, held.tile([P, 2, T], F32, name="raw%d%d" % gu)) for gu in units)

        for e in range(2):
            nc.sync.dma_start(raw[first_unit][:, e, :], x_view[0, :, e, :])
            if e == 0:
                nc.sync.dma_start(offsets[:], offs)
        for gu in units[1:]:
            g, u = gu
            for c0, cw, sc in CHUNKS[gu]:
                nc.sync.dma_start(raw[gu][:, :, c0 : c0 + cw], x_view[g, :, 2 * u : 2 * u + 2, c0 : c0 + cw])
        for e, g in halves:
            nc.sync.dma_start(w_raw[(e, g)][:], w[e].rearrange("(g p j) n -> g p j n", p=P, j=4)[g])

        window = [held.tile([P, T], F32, name="window%d" % b) for b in range(BLOCKS)]
        for b in range(BLOCKS):
            nc.vector.memset(window[b][:], 0.0)

        def gpsimd_cast(dst, src):
            nc.gpsimd.tensor_scalar(
                out=dst, in0=src, scalar1=1.0, scalar2=0.0, op0=mybir.AluOpType.mult, op1=mybir.AluOpType.add
            )

        w_grouped = [
            held.tile([P, PASSES, N, 4], BF16, name="w_grouped%d" % e, tag="w_grouped%d" % e, align_bytes=64) for e in range(E)
        ]
        w_codes = [
            held.tile([P, PASSES * N], U32, name="w_codes%d" % e, tag="w_codes%d" % e, align_bytes=64) for e in range(E)
        ]
        w_scales = [held.tile([P, PASSES * N], U8, name="w_scales%d" % e, align_bytes=64) for e in range(E)]

        def group_w(e, g):
            mine = W_SHARE if e in (0, E - 1) else N
            nc.scalar.copy(
                out=w_grouped[e][:, g, :mine].rearrange("p (c i) j -> p c j i", i=4),
                in_=w_raw[(e, g)][:, :, :mine].rearrange("p j (c i) -> p c j i", i=4),
            )
            if mine < N:
                gpsimd_cast(w_grouped[e][:, g, mine:], w_raw[(e, g)][:, :, mine:].rearrange("p j n -> p n j"))

        def quantize_w(e, g0, gn):
            nc.vector.quantize_mx(
                out=w_codes[e][:, g0 * N : (g0 + gn) * N].bitcast(FP8X4),
                scales=w_scales[e][:, g0 * N : (g0 + gn) * N],
                in_=w_grouped[e][:, g0 : g0 + gn].rearrange("p g n j -> p (g n j)"),
            )

        pair = dict((gu, held.tile([P, T, 2], BF16, name="pair%d%d" % gu)) for gu in units[1:])
        grouped = [held.tile([P, SLOTS, 4], BF16, name="grouped%d" % g, align_bytes=64) for g in range(PASSES)]
        x_codes = [held.tile([P, SLOTS], U32, name="x_codes%d" % g, align_bytes=64) for g in range(PASSES - 1)]
        x_scales = [held.tile([P, SLOTS], U8, name="x_scales%d" % g, align_bytes=64) for g in range(PASSES)]

        def codes_of(g, s0, sn):
            if g < PASSES - 1:
                return x_codes[g][:, s0 : s0 + sn]
            return x_codes_last[0][:, s0 : s0 + sn]

        def quantize_x(g, cut):
            s0, sn = cut
            nc.vector.quantize_mx(
                out=codes_of(g, s0, sn).bitcast(FP8X4),
                scales=x_scales[g][:, s0 : s0 + sn],
                in_=grouped[g][:, s0 : s0 + sn, :].rearrange("p s t -> p (s t)"),
            )

        x_codes_last = []

        for e in range(2):
            nc.vector.tensor_copy(out=grouped[0][:, :, e], in_=raw[first_unit][:, e, :].indirect(offsets[:]))
        for gu in units[1:]:
            g, u = gu
            for c0, cw, sc in CHUNKS[gu]:
                nc.scalar.copy(
                    out=pair[gu][:, c0 : c0 + sc, :],
                    in_=raw[gu][:, :, c0 : c0 + sc].rearrange("p e n -> p n e"),
                )
                if sc < cw:
                    rest = pair[gu][:, c0 + sc : c0 + cw, :]
                    planes = raw[gu][:, :, c0 + sc : c0 + cw].rearrange("p e n -> p n e")
                    gpsimd_cast(rest, planes)
            words = pair[gu][:].rearrange("p n e -> p (n e)").bitcast(U32)
            slot_words = grouped[g][:].rearrange("p s t -> p (s t)").bitcast(U32).rearrange("p (s u) -> p s u", u=2)
            nc.vector.tensor_copy(out=slot_words[:, :, u], in_=words.indirect(offsets[:]))
            if u == 1 and g < PASSES - 1:
                for cut in QUANT_CUTS[g]:
                    quantize_x(g, cut)

        acc = dict()
        y = dict()

        def multiply(e):
            for b in range(BLOCKS):
                acc[(e, b)] = psum.tile([P, C], F32, name="acc%d%d" % (e, b), tag="acc%d%d" % (1 if e == 2 else e, b))
                for g in range(PASSES):
                    cols = slice(g * N + b * P, g * N + (b + 1) * P)
                    nc.tensor.matmul_mx(
                        out=acc[(e, b)][:],
                        lhsT=w_codes[e][:, cols].bitcast(FP8X4),
                        lhsT_scale=w_scales[e][:, cols],
                        rhs=codes_of(g, e * C, C).bitcast(FP8X4),
                        rhs_scale=x_scales[g][:, e * C : (e + 1) * C],
                        start=(g == 0),
                        stop=(g == PASSES - 1),
                    )

        def copy_out(e, b, tag):
            sums = held.tile([P, C], F32, name="y%d%d" % (e, b), tag=tag)
            y[(e, b)] = sums[:]
            nc.scalar.copy(out=y[(e, b)], in_=acc[(e, b)][:])

        for g in range(PASSES):
            group_w(0, g)
        quantize_w(0, 0, PASSES)
        x_codes_last.append(held.tile([P, SLOTS], U32, name="x_codes_last", tag="w_grouped0", align_bytes=64))
        for cut in QUANT_CUTS[PASSES - 1]:
            quantize_x(PASSES - 1, cut)
        group_w(1, 0)
        multiply(0)
        copy_out(0, 0, "y00")
        group_w(1, 1)
        copy_out(0, 1, "w_raw11")
        quantize_w(1, 0, PASSES)
        group_w(2, 0)
        group_w(2, 1)
        multiply(1)
        quantize_w(2, 0, PASSES)
        group_w(3, 0)
        group_w(3, 1)
        quantize_w(3, 0, PASSES)
        sums1 = held.tile([P, BLOCKS, C], F32, name="sums1", tag="w_raw31")
        for b in range(BLOCKS):
            y[(1, b)] = sums1[:, b, :]
            nc.scalar.copy(out=y[(1, b)], in_=acc[(1, b)][:])
        multiply(2)
        multiply(3)
        for b in range(BLOCKS):
            sums23 = held.tile([P, 2 * C], F32, name="y23%d" % b)
            y[(2, b)] = sums23[:]
            for e in (2, 3):
                nc.scalar.copy(out=sums23[:, (e - 2) * C : (e - 1) * C], in_=acc[(e, b)][:])

        for first, count, b in SCATTER_ORDER:
            nc.vector.tensor_copy(
                out=window[b][:].indirect(offsets[:, first * C // 16 : (first + count) * C // 16]),
                in_=y[(first, b)],
            )
        for b in range(BLOCKS):
            nc.sync.dma_start(out[b * P : (b + 1) * P, :], window[b][:])
